import numpy as np
import ml_dtypes


def mxq(x, axis, fmt="e4m3"):
    dtype, down = {"e4m3": (ml_dtypes.float8_e4m3fn, 7), "e5m2": (ml_dtypes.float8_e5m2, 14)}[fmt]
    v = np.moveaxis(np.asarray(x, np.float32).astype(ml_dtypes.bfloat16).astype(np.float64), axis, -1)
    blocks = v.reshape(v.shape[:-1] + (-1, 32))
    amax = np.abs(blocks).max(-1, keepdims=True)
    byte = np.maximum(np.where(amax > 0, np.frexp(amax)[1] - 1 + 127, 0) - down, 1)
    scale = np.exp2(byte - 127.0)
    codes = (blocks / scale).astype(np.float32).astype(dtype).astype(np.float64)
    return np.moveaxis((codes * scale).reshape(v.shape), -1, axis)


WIDE = False


def mx_kscale(k):
    if not WIDE:
        return np.ones(k)
    levels = np.array([10, -10, 5, -5, 0])
    if k % 512:
        return np.exp2(np.random.permutation(np.resize(levels, k // 32))).repeat(32)
    a = np.empty((k // 512, 16))
    for p in range(k // 512):
        a[p, :8] = np.random.permutation(np.resize(levels, 8))
        for g in range(8):
            far = levels[np.abs(levels - a[p, g]) >= 10]
            a[p, g + 8] = far[np.random.randint(len(far))]
    return np.exp2(a.ravel()).repeat(32)


def f64(x):
    return np.asarray(x).astype(np.float64)


def striped(idx):
    return np.tile(idx.reshape(-1, 16).T, (8, 1)).astype(np.uint16)


def unstriped(offs):
    return offs[:16].T.reshape(-1).astype(np.int64)


E2M1 = np.array([0.0, 0.5, 1.0, 1.5, 2.0, 3.0, 4.0, 6.0, -0.0, -0.5, -1.0, -1.5, -2.0, -3.0, -4.0, -6.0])


def pack_weight(w, fmt):
    k, n = w.shape
    w = f64(np.asarray(w, np.float32).astype(ml_dtypes.bfloat16)).reshape(k // 32, 32, n)
    amax = np.abs(w).max(1)
    if fmt == "e4m3":
        byte = np.frexp(amax)[1] - 1 + 127 - 7
    else:
        mant, ex = np.frexp(amax / 6.0)
        byte = np.where(mant > 0.5, ex, ex - 1) + 127
    byte = np.clip(np.where(amax > 0, byte, 1), 1, 254)
    scaled = (w * np.exp2(127.0 - byte)[:, None, :]).reshape(k, n).astype(np.float32)
    by_word = np.ascontiguousarray(scaled.reshape(k // 512, 128, 4, n).transpose(0, 1, 3, 2))
    if fmt == "e4m3":
        words = by_word.astype(ml_dtypes.float8_e4m3fn).view(np.uint8)
    else:
        c = by_word.astype(ml_dtypes.float4_e2m1fn).view(np.uint8) & 0xF
        words = (c[..., 0::2] | (c[..., 1::2] << 4)).reshape(k // 512, 128, 2 * n)
    return np.ascontiguousarray(words), np.ascontiguousarray(byte.astype(np.uint8).reshape(k // 512, 16, n))


def unpack_weight(words, scales, fmt):
    g, _, n = scales.shape
    words = np.ascontiguousarray(words).reshape(g, 128, n, -1)
    if fmt == "e4m3":
        vals = words.view(ml_dtypes.float8_e4m3fn).astype(np.float64)
    else:
        nib = np.empty((g, 128, n, 4), np.uint8)
        nib[..., 0::2] = words & 0xF
        nib[..., 1::2] = words >> 4
        vals = E2M1[nib]
    vals = vals * np.repeat(np.exp2(scales.astype(np.float64) - 127.0), 8, axis=1)[..., None]
    return vals.transpose(0, 1, 3, 2).reshape(g * 512, n)


def gelu(v):
    return 0.5 * v * (1.0 + np.tanh(np.sqrt(2.0 / np.pi) * (v + 0.044715 * v**3)))


K, H, T, S, S2, T3, P = 512, 1536, 4096, 1024, 512, 2048, 512

def setup_inputs():
    n = np.random.standard_normal
    s = mx_kscale(K)[:, None]
    u = mx_kscale(H)[:, None]
    d = {}
    d["tab_words"], d["tab_scales"] = pack_weight(n((K, T)) * s, "e4m3")
    d["offs"] = striped(np.random.permutation(T)[:S])
    d["tab2_words"], d["tab2_scales"] = pack_weight(n((H, T3)) / u / H ** 0.5, "e4m3")
    d["offs2"] = striped(np.random.permutation(T3)[:S2])
    d["pos1"] = striped(np.random.permutation(S)[:P])
    d["pos2"] = striped(np.random.permutation(S)[:P])
    d["w1"] = (1.4 * n((K, H)) / s * u.T / K ** 0.5).astype(np.float32)
    d["w4_words"], d["w4_scales"] = pack_weight(0.8 * n((K, H)) / s * u.T / K ** 0.5, "e2m1")
    d["cap"] = (np.random.uniform(0.6, 1.6, H) * u[:, 0]).astype(np.float32)
    d["base"] = np.random.uniform(0.6, 1.6, S2).astype(np.float32)
    return d

def reference(tab_words, tab_scales, offs, tab2_words, tab2_scales, offs2, pos1, pos2,
              w1, w4_words, w4_scales, cap, base):
    v = unpack_weight(tab_words, tab_scales, "e4m3")[:, unstriped(offs)]
    v2 = unpack_weight(tab2_words, tab2_scales, "e4m3")[:, unstriped(offs2)]
    w4 = unpack_weight(w4_words, w4_scales, "e2m1")
    a = np.minimum(np.abs(mxq(f64(w1), 0, "e4m3").T @ v), f64(cap)[:, None])
    h = a + (w4.T @ v)
    e = v2.T @ mxq(h, 0, "e4m3")
    e1 = e[:, unstriped(pos1)]
    e2 = e[:, unstriped(pos2)]
    return (e1 + e2) / (f64(base)[:, None] + np.abs(e1))

@@ -1,0 +1,240 @@
+from contextlib import ExitStack
+
+import concourse.mybir as mybir
+
+K, H, T, S, S2, T3, NP = 512, 1536, 4096, 1024, 512, 2048, 512
+FLOPS = 2 * (2 * K * H * S + H * S2 * S)
+
+F32 = mybir.dt.float32
+BF16 = mybir.dt.bfloat16
+I32 = mybir.dt.int32
+U32 = mybir.dt.uint32
+U16 = mybir.dt.uint16
+U8 = mybir.dt.uint8
+FP8X4 = mybir.dt.float8_e4m3fn_x4
+FP4X4 = mybir.dt.float4_e2m1fn_x4
+ALU = mybir.AluOpType
+ACT = mybir.ActivationFunctionType
+
+P = 128
+PACK = 4
+N = 512
+CHUNKS = H // N
+HALVES = S // N
+MT = S2 // P
+SC_COLS = [176, 176, 176, 176, 288, 176]
+LEAD = 2
+
+
+def tile_list_bottle_fault_tracing_kernel(tc, tab_words, tab_scales, offs, tab2_words, tab2_scales, offs2,
+                                                   pos1, pos2, w1, w4_words, w4_scales, cap, base, out):
+    nc = tc.nc
+    with ExitStack() as ctx:
+        lists = ctx.enter_context(tc.tile_pool(name="lists", bufs=1))
+        keep = ctx.enter_context(tc.tile_pool(name="keep", bufs=1))
+        ring = ctx.enter_context(tc.tile_pool(name="ring", bufs=2))
+        ring3 = ctx.enter_context(tc.tile_pool(name="ring3", bufs=4))
+        psab = ctx.enter_context(tc.psum_pool(name="psab", bufs=3))
+        pse = ctx.enter_context(tc.psum_pool(name="pse", bufs=1))
+
+        idx = lists.tile([P, S // 16], U16, name="idx")
+        idx2 = lists.tile([P, S2 // 16], U16, name="idx2")
+        p1 = lists.tile([P, NP // 16], U16, name="p1")
+        p2 = lists.tile([P, NP // 16], U16, name="p2")
+
+        tabw = keep.tile([P, T], I32, name="tabw", align_bytes=64)
+        tabs = keep.tile([P, T], U8, name="tabs", align_bytes=64)
+        tab2w = [keep.tile([P, T3], I32, name=f"tab2w{a}", align_bytes=64) for a in range(CHUNKS)]
+        tab2s = keep.tile([P, T3], U8, name="tab2s", align_bytes=64)
+        w4raw = keep.tile([P, 2 * H], U8, name="w4raw", align_bytes=64)
+        w4sraw = keep.tile([P, H], U8, name="w4sraw", align_bytes=64)
+        capt = keep.tile([P, CHUNKS, PACK], F32, name="capt")
+        baset = keep.tile([P, MT], F32, name="baset")
+        warm = keep.tile([P, 8], F32, name="warm")
+        warm2 = keep.tile([P, 8], F32, name="warm2")
+
+        nc.vector.memset(tabs[:].bitcast(I32), 0)
+        nc.vector.memset(w4sraw[:].bitcast(I32), 0)
+        nc.vector.memset(tab2s[:].bitcast(I32), 0)
+        nc.vector.memset(warm[:], 1.0)
+        nc.scalar.activation(warm2[:], warm[:], ACT.Abs_reciprocal_sqrt)
+
+        nc.sync.dma_start(idx[:], offs)
+        for q in range(4):
+            nc.sync.dma_start(tabs[32 * q:32 * q + 4, :].bitcast(I32), tab_scales[0, 4 * q:4 * q + 4, :].bitcast(I32))
+        nc.sync.dma_start(w4raw[:].bitcast(I32), w4_words[0].bitcast(I32))
+        nc.sync.dma_start(tabw[:], tab_words[0].rearrange("p n t -> p (n t)").bitcast(I32))
+        w1v = w1.rearrange("(p j) c -> p j c", j=PACK)
+        w1raw0 = [keep.tile([P, PACK, N // 2], F32, name=f"w1raw0_{u}") for u in range(2)]
+        w1raw = [None] + [keep.tile([P, PACK, N], F32, name=f"w1raw{a}") for a in range(1, CHUNKS)]
+        nc.sync.dma_start(w1raw0[0][:], w1v[:, :, 0:N // 2])
+        for q in range(4):
+            nc.scalar.dma_start(w4sraw[32 * q:32 * q + 4, :].bitcast(I32), w4_scales[0, 4 * q:4 * q + 4, :].bitcast(I32))
+        nc.sync.dma_start(w1raw0[1][:], w1v[:, :, N // 2:N])
+        nc.sync.dma_start(capt[:], cap.rearrange("(a p t) -> p a t", p=P, t=PACK))
+        nc.sync.dma_start(idx2[:], offs2)
+        for q in range(4):
+            nc.sync.dma_start(tab2s[32 * q:32 * q + 4 * CHUNKS, :].bitcast(I32),
+                              tab2_scales[:, 4 * q:4 * q + 4, :].bitcast(I32))
+        for a in range(CHUNKS):
+            if a + 1 < CHUNKS:
+                nc.sync.dma_start(w1raw[a + 1][:], w1v[:, :, (a + 1) * N:(a + 2) * N])
+            nc.sync.dma_start(tab2w[a][:], tab2_words[a].rearrange("p n t -> p (n t)").bitcast(I32))
+        nc.sync.dma_start(p1[:], pos1)
+        nc.sync.dma_start(p2[:], pos2)
+        with nc.allow_non_contiguous_dma(reason="one value a partition"):
+            nc.sync.dma_start(baset[:], base.rearrange("(m p) -> p m", p=P))
+
+        vs = keep.tile([P, S], U8, name="vs", align_bytes=64)
+        vw = [keep.tile([P, N], U32, name=f"vw{j}", align_bytes=64) for j in range(HALVES)]
+        w4d = [keep.tile([P, 2 * N], U8, name=f"w4d{a}", align_bytes=64) for a in range(CHUNKS)]
+        w4sd = [keep.tile([P, N], U8, name=f"w4sd{a}", align_bytes=64) for a in range(CHUNKS)]
+        w1q = [keep.tile([P, N], U32, name=f"w1q{a}", align_bytes=64) for a in range(CHUNKS)]
+        w1s = [keep.tile([P, N], U8, name=f"w1s{a}", align_bytes=64) for a in range(CHUNKS)]
+        w1b = [keep.tile([P, PACK * N], BF16, name=f"w1b{a}", align_bytes=64) for a in range(CHUNKS)]
+        v2w = [[keep.tile([P, S2 // 2], U32, name=f"v2w{u}_{a}", align_bytes=64) for a in range(CHUNKS)]
+               for u in range(2)]
+        v2s = keep.tile([P, S2], U8, name="v2s", align_bytes=64)
+        hq = [[keep.tile([P, N], U32, name=f"hq{j}_{a}", align_bytes=64) for a in range(CHUNKS)] for j in range(HALVES)]
+        hs = [[keep.tile([P, N], U8, name=f"hs{j}_{a}", align_bytes=64) for a in range(CHUNKS)] for j in range(HALVES)]
+        scores = [keep.tile([P, S], F32, name=f"scores{m}", align_bytes=64) for m in range(MT)]
+
+        def deal_w4(a):
+            nc.vector.tensor_copy(w4d[a][:].rearrange("p (t q b) -> p t q b", t=PACK, b=2),
+                                  w4raw[:, 2 * N * a:2 * N * (a + 1)].rearrange("p (q t b) -> p t q b", t=PACK, b=2))
+            nc.vector.tensor_copy(w4sd[a][:].rearrange("p (t q) -> p t q", t=PACK),
+                                  w4sraw[:, N * a:N * (a + 1)].rearrange("p (q t) -> p t q", t=PACK))
+
+        def cast_w1(a, raw, m0, mn):
+            dst = w1b[a][:].rearrange("p (t m j) -> p m j t", t=PACK, j=PACK)[:, m0:m0 + mn]
+            nc.scalar.copy(dst, raw.rearrange("p j (m t) -> p m j t", t=PACK))
+
+        def quant_w1(a):
+            nc.vector.quantize_mx(out=w1q[a][:].bitcast(FP8X4), scales=w1s[a][:], in_=w1b[a][:])
+
+        def gather_v2(u, a):
+            nc.vector.tensor_copy(v2w[u][a][:], tab2w[a][:].bitcast(U32).indirect(idx2[:, 16 * u:16 * (u + 1)]))
+
+        nc.vector.tensor_copy(vs[:], tabs[:].indirect(idx[:]))
+        deal_w4(0)
+        for j in range(HALVES):
+            nc.vector.tensor_copy(vw[j][:], tabw[:].bitcast(U32).indirect(idx[:, 32 * j:32 * (j + 1)]))
+        for u in range(2):
+            cast_w1(0, w1raw0[u][:], u * 64, 64)
+        quant_w1(0)
+        for a in range(1, CHUNKS):
+            deal_w4(a)
+        nc.vector.tensor_copy(v2s[:], tab2s[:].indirect(idx2[:]))
+
+        units = [(j, a) for a in range(CHUNKS) for j in range(HALVES)]
+        steps = [(j, a, t) for j, a in units for t in range(PACK)]
+        mags, hbs, his, banks = {}, {}, {}, {}
+
+        def contrast(s):
+            j, a, t = steps[s]
+            pa = psab.tile([P, N], F32, name="pa")
+            nc.tensor.matmul_mx(out=pa[:], lhsT=w1q[a][:, t * P:(t + 1) * P].bitcast(FP8X4),
+                                lhsT_scale=w1s[a][:, t * P:(t + 1) * P],
+                                rhs=vw[j][:].bitcast(FP8X4), rhs_scale=vs[:, j * N:(j + 1) * N],
+                                start=True, stop=True)
+            mags[s] = ring3.tile([P, N], F32, name="mag")
+            nc.scalar.activation(mags[s][:], pa[:], ACT.Abs)
+
+        def residual(s):
+            j, a, t = steps[s]
+            if t == 0:
+                hbs[j, a] = ring.tile([P, PACK, N], BF16, name="hb", align_bytes=64)
+            pb = psab.tile([P, N], F32, name="pb")
+            nc.tensor.matmul_mx(out=pb[:], lhsT=w4d[a][:, 2 * t * P:2 * (t + 1) * P].bitcast(FP4X4),
+                                lhsT_scale=w4sd[a][:, t * P:(t + 1) * P],
+                                rhs=vw[j][:].bitcast(FP8X4), rhs_scale=vs[:, j * N:(j + 1) * N],
+                                start=True, stop=True)
+            nc.vector.scalar_tensor_tensor(hbs[j, a][:, t, :], mags[s][:], capt[:, a, t:t + 1], pb[:],
+                                           ALU.min, ALU.add)
+
+        def weave(eng, u):
+            j, a = units[u]
+            if (j, a) not in his:
+                his[j, a] = ring.tile([P, N, PACK], BF16, name="hi", align_bytes=64)
+            src = hbs[j, a][:].rearrange("p t (c i) -> p c t i", i=4)
+            dst = his[j, a][:].rearrange("p (c i) t -> p c t i", i=4)
+            cut = SC_COLS[u] // 4
+            if eng == "s":
+                nc.scalar.copy(dst[:, 0:cut], src[:, 0:cut])
+            else:
+                nc.vector.tensor_copy(dst[:, cut:N // 4], src[:, cut:N // 4])
+
+        def quant_h(u):
+            j, a = units[u]
+            nc.vector.quantize_mx(out=hq[j][a][:].bitcast(FP8X4), scales=hs[j][a][:],
+                                  in_=his[j, a][:].rearrange("p n t -> p (n t)"))
+
+        def score_pass(j, a, m):
+            if a == 0:
+                banks[j, m] = pse.tile([P, N], F32, name=f"e{j}")
+            u, c = divmod(m * P, S2 // 2)
+            nc.tensor.matmul_mx(out=banks[j, m][:], lhsT=v2w[u][a][:, c:c + P].bitcast(FP8X4),
+                                lhsT_scale=v2s[4 * a:P, m * P:(m + 1) * P],
+                                rhs=hq[j][a][:].bitcast(FP8X4), rhs_scale=hs[j][a][:],
+                                start=(a == 0), stop=(a == CHUNKS - 1))
+            if a == CHUNKS - 1:
+                nc.scalar.copy(scores[m][:, j * N:(j + 1) * N], banks[j, m][:])
+
+        for s in range(LEAD):
+            contrast(s)
+        for s in range(len(steps)):
+            u, t = divmod(s, PACK)
+            j, a = units[u]
+            if s + LEAD < len(steps):
+                contrast(s + LEAD)
+            if u > 0 and t == 0:
+                weave("s", u - 1)
+            residual(s)
+            if a + 1 < CHUNKS and j == 0:
+                cast_w1(a + 1, w1raw[a + 1][:, :, t * P:(t + 1) * P], t * 32, 32)
+            if a + 1 < CHUNKS and j == 1 and t == 0:
+                quant_w1(a + 1)
+            if u > 0 and t == 0:
+                weave("v", u - 1)
+            if u > 0 and t == 1:
+                quant_h(u - 1)
+                pj, pa_ = units[u - 1]
+                if pj == 0:
+                    gather_v2(0, pa_)
+                score_pass(pj, pa_, 0)
+        last = len(units) - 1
+        weave("s", last)
+        weave("v", last)
+        gather_v2(1, 0)
+        quant_h(last)
+        score_pass(1, CHUNKS - 1, 0)
+        for a in range(1, CHUNKS):
+            gather_v2(1, a)
+
+        tiles = {}
+
+        def shoulder(m):
+            e1 = ring.tile([P, NP], F32, name="e1")
+            mag1 = ring.tile([P, NP], F32, name="mag1")
+            root = ring.tile([P, NP], F32, name="root")
+            inv = ring.tile([P, NP], F32, name="inv")
+            nc.vector.tensor_copy(e1[:], scores[m][:].indirect(p1[:]))
+            nc.scalar.activation(mag1[:], e1[:], ACT.Abs)
+            nc.scalar.activation(root[:], mag1[:], ACT.Abs_reciprocal_sqrt, bias=baset[:, m:m + 1])
+            nc.scalar.activation(inv[:], root[:], ACT.Square)
+            tiles[m] = (e1, inv)
+
+        shoulder(0)
+        for m in range(MT):
+            e1, inv = tiles[m]
+            tot = ring.tile([P, NP], F32, name="tot")
+            res = ring.tile([P, NP], F32, name="res")
+            if m + 1 < MT:
+                for j in range(HALVES):
+                    for a in range(CHUNKS):
+                        score_pass(j, a, m + 1)
+            nc.vector.tensor_tensor(tot[:], scores[m][:].indirect(p2[:]), e1[:], ALU.add)
+            if m + 1 < MT:
+                shoulder(m + 1)
+            nc.vector.tensor_tensor(res[:], tot[:], inv[:], ALU.mult)
+            nc.sync.dma_start(out[m * P:(m + 1) * P, :], res[:])

@@ -22,7 +22,7 @@ N = 512
 CHUNKS = H // N
 HALVES = S // N
 MT = S2 // P
-SC_COLS = [176, 176, 176, 176, 288, 176]
+SC_COLS = [128, 128, 128, 128, 128, 176]
 LEAD = 2
 
 
@@ -42,50 +42,34 @@ def tile_list_bottle_fault_tracing_kernel(tc, tab_words, tab_scales, offs, tab2_
         p1 = lists.tile([P, NP // 16], U16, name="p1")
         p2 = lists.tile([P, NP // 16], U16, name="p2")
 
-        tabw = keep.tile([P, T], I32, name="tabw", align_bytes=64)
+        over = ctx.enter_context(tc.tile_pool(name="over", bufs=1))
         tabs = keep.tile([P, T], U8, name="tabs", align_bytes=64)
-        tab2w = [keep.tile([P, T3], I32, name=f"tab2w{a}", align_bytes=64) for a in range(CHUNKS)]
-        tab2s = keep.tile([P, T3], U8, name="tab2s", align_bytes=64)
-        w4raw = keep.tile([P, 2 * H], U8, name="w4raw", align_bytes=64)
-        w4sraw = keep.tile([P, H], U8, name="w4sraw", align_bytes=64)
-        capt = keep.tile([P, CHUNKS, PACK], F32, name="capt")
-        baset = keep.tile([P, MT], F32, name="baset")
-        warm = keep.tile([P, 8], F32, name="warm")
+        w4raw = keep.tile([P, 2 * H], U8, name="w4raw", tag="w4raw", align_bytes=64)
+        warm = over.tile([P, 8], F32, name="warm", offset=0)
         warm2 = keep.tile([P, 8], F32, name="warm2")
 
         nc.vector.memset(tabs[:].bitcast(I32), 0)
-        nc.vector.memset(w4sraw[:].bitcast(I32), 0)
-        nc.vector.memset(tab2s[:].bitcast(I32), 0)
-        nc.vector.memset(warm[:], 1.0)
+        nc.gpsimd.memset(warm[:], 1.0)
         nc.scalar.activation(warm2[:], warm[:], ACT.Abs_reciprocal_sqrt)
 
-        nc.sync.dma_start(idx[:], offs)
-        for q in range(4):
-            nc.sync.dma_start(tabs[32 * q:32 * q + 4, :].bitcast(I32), tab_scales[0, 4 * q:4 * q + 4, :].bitcast(I32))
-        nc.sync.dma_start(w4raw[:].bitcast(I32), w4_words[0].bitcast(I32))
-        nc.sync.dma_start(tabw[:], tab_words[0].rearrange("p n t -> p (n t)").bitcast(I32))
         w1v = w1.rearrange("(p j) c -> p j c", j=PACK)
-        w1raw0 = [keep.tile([P, PACK, N // 2], F32, name=f"w1raw0_{u}") for u in range(2)]
-        w1raw = [None] + [keep.tile([P, PACK, N], F32, name=f"w1raw{a}") for a in range(1, CHUNKS)]
-        nc.sync.dma_start(w1raw0[0][:], w1v[:, :, 0:N // 2])
-        for q in range(4):
-            nc.scalar.dma_start(w4sraw[32 * q:32 * q + 4, :].bitcast(I32), w4_scales[0, 4 * q:4 * q + 4, :].bitcast(I32))
-        nc.sync.dma_start(w1raw0[1][:], w1v[:, :, N // 2:N])
-        nc.sync.dma_start(capt[:], cap.rearrange("(a p t) -> p a t", p=P, t=PACK))
+        w1first = [keep.tile([P, PACK, N // 2], F32, name=f"w1first{u}", tag=f"w1first{u}") for u in range(2)]
+        w1second = keep.tile([P, PACK, N], F32, name="w1second", tag="w1second")
+        tabw = over.tile([P, T], I32, name="tabw", offset=0)
+
+        nc.sync.dma_start(w4raw[:].bitcast(I32), w4_words[0].bitcast(I32))
+        nc.sync.dma_start(idx[:], offs)
         nc.sync.dma_start(idx2[:], offs2)
-        for q in range(4):
-            nc.sync.dma_start(tab2s[32 * q:32 * q + 4 * CHUNKS, :].bitcast(I32),
-                              tab2_scales[:, 4 * q:4 * q + 4, :].bitcast(I32))
-        for a in range(CHUNKS):
-            if a + 1 < CHUNKS:
-                nc.sync.dma_start(w1raw[a + 1][:], w1v[:, :, (a + 1) * N:(a + 2) * N])
-            nc.sync.dma_start(tab2w[a][:], tab2_words[a].rearrange("p n t -> p (n t)").bitcast(I32))
         nc.sync.dma_start(p1[:], pos1)
         nc.sync.dma_start(p2[:], pos2)
-        with nc.allow_non_contiguous_dma(reason="one value a partition"):
-            nc.sync.dma_start(baset[:], base.rearrange("(m p) -> p m", p=P))
+        for u in range(2):
+            nc.sync.dma_start(w1first[u][:], w1v[:, :, u * (N // 2):(u + 1) * (N // 2)])
+        nc.sync.dma_start(w1second[:], w1v[:, :, N:2 * N])
+        for q in range(4):
+            nc.sync.dma_start(tabs[32 * q:32 * q + 4, :].bitcast(I32), tab_scales[0, 4 * q:4 * q + 4, :].bitcast(I32))
+        nc.sync.dma_start(tabw[:], tab_words[0].rearrange("p n t -> p (n t)").bitcast(I32))
 
-        vs = keep.tile([P, S], U8, name="vs", align_bytes=64)
+        vs = [keep.tile([P, N], U8, name=f"vs{j}", align_bytes=64) for j in range(HALVES)]
         vw = [keep.tile([P, N], U32, name=f"vw{j}", align_bytes=64) for j in range(HALVES)]
         w4d = [keep.tile([P, 2 * N], U8, name=f"w4d{a}", align_bytes=64) for a in range(CHUNKS)]
         w4sd = [keep.tile([P, N], U8, name=f"w4sd{a}", align_bytes=64) for a in range(CHUNKS)]
@@ -99,9 +83,11 @@ def tile_list_bottle_fault_tracing_kernel(tc, tab_words, tab_scales, offs, tab2_
         hs = [[keep.tile([P, N], U8, name=f"hs{j}_{a}", align_bytes=64) for a in range(CHUNKS)] for j in range(HALVES)]
         scores = [keep.tile([P, S], F32, name=f"scores{m}", align_bytes=64) for m in range(MT)]
 
-        def deal_w4(a):
+        def deal_words(a):
             nc.vector.tensor_copy(w4d[a][:].rearrange("p (t q b) -> p t q b", t=PACK, b=2),
                                   w4raw[:, 2 * N * a:2 * N * (a + 1)].rearrange("p (q t b) -> p t q b", t=PACK, b=2))
+
+        def deal_scales(a):
             nc.vector.tensor_copy(w4sd[a][:].rearrange("p (t q) -> p t q", t=PACK),
                                   w4sraw[:, N * a:N * (a + 1)].rearrange("p (q t) -> p t q", t=PACK))
 
@@ -113,18 +99,43 @@ def tile_list_bottle_fault_tracing_kernel(tc, tab_words, tab_scales, offs, tab2_
             nc.vector.quantize_mx(out=w1q[a][:].bitcast(FP8X4), scales=w1s[a][:], in_=w1b[a][:])
 
         def gather_v2(u, a):
-            nc.vector.tensor_copy(v2w[u][a][:], tab2w[a][:].bitcast(U32).indirect(idx2[:, 16 * u:16 * (u + 1)]))
+            nc.vector.tensor_copy(v2w[u][a][:], tab2w[:, a * T3:(a + 1) * T3].bitcast(U32).indirect(idx2[:, 16 * u:16 * (u + 1)]))
 
-        nc.vector.tensor_copy(vs[:], tabs[:].indirect(idx[:]))
-        deal_w4(0)
+        for a in range(CHUNKS):
+            deal_words(a)
+        w4sraw = keep.tile([P, H], U8, name="w4sraw", tag="w4raw", align_bytes=64)
+        nc.vector.memset(w4sraw[:].bitcast(I32), 0)
+        for q in range(4):
+            nc.sync.dma_start(w4sraw[32 * q:32 * q + 4, :].bitcast(I32), w4_scales[0, 4 * q:4 * q + 4, :].bitcast(I32))
+        for u in range(2):
+            cast_w1(0, w1first[u][:], u * 64, 64)
+        capt = keep.tile([P, CHUNKS, PACK], F32, name="capt", tag="w1first0")
+        nc.sync.dma_start(capt[:], cap.rearrange("(a p t) -> p a t", p=P, t=PACK))
+        quant_w1(0)
+        cast_w1(1, w1second[:], 0, P)
+        w1third = keep.tile([P, PACK, N], F32, name="w1third", tag="w1second")
+        nc.sync.dma_start(w1third[:], w1v[:, :, 2 * N:3 * N])
+        for j in range(HALVES):
+            nc.vector.tensor_copy(vs[j][:], tabs[:].indirect(idx[:, 32 * j:32 * (j + 1)]))
         for j in range(HALVES):
             nc.vector.tensor_copy(vw[j][:], tabw[:].bitcast(U32).indirect(idx[:, 32 * j:32 * (j + 1)]))
-        for u in range(2):
-            cast_w1(0, w1raw0[u][:], u * 64, 64)
-        quant_w1(0)
+            if j == 0:
+                deal_scales(0)
+        quant_w1(1)
         for a in range(1, CHUNKS):
-            deal_w4(a)
-        nc.vector.tensor_copy(v2s[:], tab2s[:].indirect(idx2[:]))
+            deal_scales(a)
+
+        tab2s = over.tile([P, T3], U8, name="tab2s", offset=0)
+        tab2w = over.tile([P, CHUNKS * T3], I32, name="tab2w", offset=T3 + 64)
+        nc.vector.memset(tab2s[:].bitcast(I32), 0)
+        for q in range(4):
+            nc.sync.dma_start(tab2s[32 * q:32 * q + 4 * CHUNKS, :].bitcast(I32),
+                              tab2_scales[:, 4 * q:4 * q + 4, :].bitcast(I32))
+        nc.sync.dma_start(tab2w[:].rearrange("p (a n) -> p a n", a=CHUNKS),
+                          tab2_words.rearrange("a p n t -> p a (n t)").bitcast(I32))
+        baset = over.tile([P, MT], F32, name="baset", offset=T3)
+        with nc.allow_non_contiguous_dma(reason="one value a partition"):
+            nc.sync.dma_start(baset[:], base.rearrange("(m p) -> p m", p=P))
 
         units = [(j, a) for a in range(CHUNKS) for j in range(HALVES)]
         steps = [(j, a, t) for j, a in units for t in range(PACK)]
@@ -135,7 +146,7 @@ def tile_list_bottle_fault_tracing_kernel(tc, tab_words, tab_scales, offs, tab2_
             pa = psab.tile([P, N], F32, name="pa")
             nc.tensor.matmul_mx(out=pa[:], lhsT=w1q[a][:, t * P:(t + 1) * P].bitcast(FP8X4),
                                 lhsT_scale=w1s[a][:, t * P:(t + 1) * P],
-                                rhs=vw[j][:].bitcast(FP8X4), rhs_scale=vs[:, j * N:(j + 1) * N],
+                                rhs=vw[j][:].bitcast(FP8X4), rhs_scale=vs[j][:],
                                 start=True, stop=True)
             mags[s] = ring3.tile([P, N], F32, name="mag")
             nc.scalar.activation(mags[s][:], pa[:], ACT.Abs)
@@ -147,7 +158,7 @@ def tile_list_bottle_fault_tracing_kernel(tc, tab_words, tab_scales, offs, tab2_
             pb = psab.tile([P, N], F32, name="pb")
             nc.tensor.matmul_mx(out=pb[:], lhsT=w4d[a][:, 2 * t * P:2 * (t + 1) * P].bitcast(FP4X4),
                                 lhsT_scale=w4sd[a][:, t * P:(t + 1) * P],
-                                rhs=vw[j][:].bitcast(FP8X4), rhs_scale=vs[:, j * N:(j + 1) * N],
+                                rhs=vw[j][:].bitcast(FP8X4), rhs_scale=vs[j][:],
                                 start=True, stop=True)
             nc.vector.scalar_tensor_tensor(hbs[j, a][:, t, :], mags[s][:], capt[:, a, t:t + 1], pb[:],
                                            ALU.min, ALU.add)
@@ -155,14 +166,20 @@ def tile_list_bottle_fault_tracing_kernel(tc, tab_words, tab_scales, offs, tab2_
         def weave(eng, u):
             j, a = units[u]
             if (j, a) not in his:
-                his[j, a] = ring.tile([P, N, PACK], BF16, name="hi", align_bytes=64)
+                his[j, a] = keep.tile([P, N, PACK], BF16, name="hi" if u + 1 < len(units) else "hi_last",
+                                      align_bytes=64)
             src = hbs[j, a][:].rearrange("p t (c i) -> p c t i", i=4)
             dst = his[j, a][:].rearrange("p (c i) t -> p c t i", i=4)
             cut = SC_COLS[u] // 4
             if eng == "s":
-                nc.scalar.copy(dst[:, 0:cut], src[:, 0:cut])
-            else:
+                if cut > 0:
+                    nc.scalar.copy(dst[:, 0:cut], src[:, 0:cut])
+            elif eng == "v":
                 nc.vector.tensor_copy(dst[:, cut:N // 4], src[:, cut:N // 4])
+            else:
+                nc.gpsimd.tensor_scalar(his[j, a][:, 4 * cut:N, :],
+                                        hbs[j, a][:].rearrange("p t n -> p n t")[:, 4 * cut:N, :],
+                                        1.0, 0.0, ALU.mult, ALU.add)
 
         def quant_h(u):
             j, a = units[u]
@@ -188,20 +205,32 @@ def tile_list_bottle_fault_tracing_kernel(tc, tab_words, tab_scales, offs, tab2_
             if s + LEAD < len(steps):
                 contrast(s + LEAD)
             if u > 0 and t == 0:
+                weave("g", u - 1)
                 weave("s", u - 1)
             residual(s)
-            if a + 1 < CHUNKS and j == 0:
-                cast_w1(a + 1, w1raw[a + 1][:, :, t * P:(t + 1) * P], t * 32, 32)
-            if a + 1 < CHUNKS and j == 1 and t == 0:
-                quant_w1(a + 1)
-            if u > 0 and t == 0:
-                weave("v", u - 1)
-            if u > 0 and t == 1:
-                quant_h(u - 1)
-                pj, pa_ = units[u - 1]
-                if pj == 0:
-                    gather_v2(0, pa_)
-                score_pass(pj, pa_, 0)
+            if s in (4, 6, 8, 10):
+                piece = s // 2 - 2
+                cast_w1(2, w1third[:, :, piece * P:(piece + 1) * P], piece * 32, 32)
+            if t == PACK - 1:
+                if u == 1:
+                    nc.vector.tensor_copy(v2s[:], tab2s[:].indirect(idx2[:]))
+                if u == 2:
+                    quant_w1(2)
+                if u == 3:
+                    gather_v2(0, 0)
+                    gather_v2(0, 1)
+                if u == 4:
+                    gather_v2(0, 2)
+                if u > 0:
+                    quant_h(u - 1)
+                if u == 3:
+                    score_pass(0, 0, 0)
+                    score_pass(1, 0, 0)
+                    score_pass(0, 1, 0)
+                if u == 4:
+                    score_pass(1, 1, 0)
+                if u == 5:
+                    score_pass(0, 2, 0)
         last = len(units) - 1
         weave("s", last)
         weave("v", last)

@@ -22,8 +22,9 @@ N = 512
 CHUNKS = H // N
 HALVES = S // N
 MT = S2 // P
-SC_COLS = [128, 128, 128, 128, 128, 176]
-LEAD = 2
+SC_COLS = [192, 192, 192, 192, 192, 176]
+LEAD = 3
+CASTS = [0, 1, 2, 3, 5, 6, 9, 10]
 
 
 def tile_list_bottle_fault_tracing_kernel(tc, tab_words, tab_scales, offs, tab2_words, tab2_scales, offs2,
@@ -33,7 +34,7 @@ def tile_list_bottle_fault_tracing_kernel(tc, tab_words, tab_scales, offs, tab2_
         lists = ctx.enter_context(tc.tile_pool(name="lists", bufs=1))
         keep = ctx.enter_context(tc.tile_pool(name="keep", bufs=1))
         ring = ctx.enter_context(tc.tile_pool(name="ring", bufs=2))
-        ring3 = ctx.enter_context(tc.tile_pool(name="ring3", bufs=4))
+        ring3 = ctx.enter_context(tc.tile_pool(name="ring3", bufs=5))
         psab = ctx.enter_context(tc.psum_pool(name="psab", bufs=3))
         pse = ctx.enter_context(tc.psum_pool(name="pse", bufs=1))
 
@@ -53,8 +54,7 @@ def tile_list_bottle_fault_tracing_kernel(tc, tab_words, tab_scales, offs, tab2_
         nc.scalar.activation(warm2[:], warm[:], ACT.Abs_reciprocal_sqrt)
 
         w1v = w1.rearrange("(p j) c -> p j c", j=PACK)
-        w1first = [keep.tile([P, PACK, N // 2], F32, name=f"w1first{u}", tag=f"w1first{u}") for u in range(2)]
-        w1second = keep.tile([P, PACK, N], F32, name="w1second", tag="w1second")
+        w1first = [keep.tile([P, PACK, N // 2], F32, name=f"w1first{u}", tag=f"w1first{u}", align_bytes=64) for u in range(2)]
         tabw = over.tile([P, T], I32, name="tabw", offset=0)
 
         nc.sync.dma_start(w4raw[:].bitcast(I32), w4_words[0].bitcast(I32))
@@ -64,7 +64,6 @@ def tile_list_bottle_fault_tracing_kernel(tc, tab_words, tab_scales, offs, tab2_
         nc.sync.dma_start(p2[:], pos2)
         for u in range(2):
             nc.sync.dma_start(w1first[u][:], w1v[:, :, u * (N // 2):(u + 1) * (N // 2)])
-        nc.sync.dma_start(w1second[:], w1v[:, :, N:2 * N])
         for q in range(4):
             nc.sync.dma_start(tabs[32 * q:32 * q + 4, :].bitcast(I32), tab_scales[0, 4 * q:4 * q + 4, :].bitcast(I32))
         nc.sync.dma_start(tabw[:], tab_words[0].rearrange("p n t -> p (n t)").bitcast(I32))
@@ -75,7 +74,7 @@ def tile_list_bottle_fault_tracing_kernel(tc, tab_words, tab_scales, offs, tab2_
         w4sd = [keep.tile([P, N], U8, name=f"w4sd{a}", align_bytes=64) for a in range(CHUNKS)]
         w1q = [keep.tile([P, N], U32, name=f"w1q{a}", align_bytes=64) for a in range(CHUNKS)]
         w1s = [keep.tile([P, N], U8, name=f"w1s{a}", align_bytes=64) for a in range(CHUNKS)]
-        w1b = [keep.tile([P, PACK * N], BF16, name=f"w1b{a}", align_bytes=64) for a in range(CHUNKS)]
+        w1b = [keep.tile([P, PACK * N], BF16, name=f"w1b{a}", tag=f"w1b{a}", align_bytes=64) for a in range(CHUNKS)]
         v2w = [[keep.tile([P, S2 // 2], U32, name=f"v2w{u}_{a}", align_bytes=64) for a in range(CHUNKS)]
                for u in range(2)]
         v2s = keep.tile([P, S2], U8, name="v2s", align_bytes=64)
@@ -109,19 +108,19 @@ def tile_list_bottle_fault_tracing_kernel(tc, tab_words, tab_scales, offs, tab2_
             nc.sync.dma_start(w4sraw[32 * q:32 * q + 4, :].bitcast(I32), w4_scales[0, 4 * q:4 * q + 4, :].bitcast(I32))
         for u in range(2):
             cast_w1(0, w1first[u][:], u * 64, 64)
-        capt = keep.tile([P, CHUNKS, PACK], F32, name="capt", tag="w1first0")
+        capt = keep.tile([P, CHUNKS, PACK], F32, name="capt", tag="w1first0", align_bytes=64)
         nc.sync.dma_start(capt[:], cap.rearrange("(a p t) -> p a t", p=P, t=PACK))
         quant_w1(0)
-        cast_w1(1, w1second[:], 0, P)
-        w1third = keep.tile([P, PACK, N], F32, name="w1third", tag="w1second")
-        nc.sync.dma_start(w1third[:], w1v[:, :, 2 * N:3 * N])
+        w1rest = {a: keep.tile([P, PACK, N], F32, name=f"w1rest{a}", tag=tag, align_bytes=64)
+                  for a, tag in ((1, "w1first1"), (2, "w1b0"))}
+        for a in w1rest:
+            nc.sync.dma_start(w1rest[a][:], w1v[:, :, a * N:(a + 1) * N])
         for j in range(HALVES):
             nc.vector.tensor_copy(vs[j][:], tabs[:].indirect(idx[:, 32 * j:32 * (j + 1)]))
         for j in range(HALVES):
             nc.vector.tensor_copy(vw[j][:], tabw[:].bitcast(U32).indirect(idx[:, 32 * j:32 * (j + 1)]))
             if j == 0:
                 deal_scales(0)
-        quant_w1(1)
         for a in range(1, CHUNKS):
             deal_scales(a)
 
@@ -208,14 +207,14 @@ def tile_list_bottle_fault_tracing_kernel(tc, tab_words, tab_scales, offs, tab2_
                 weave("g", u - 1)
                 weave("s", u - 1)
             residual(s)
-            if s in (4, 6, 8, 10):
-                piece = s // 2 - 2
-                cast_w1(2, w1third[:, :, piece * P:(piece + 1) * P], piece * 32, 32)
+            if s in CASTS:
+                ca, piece = divmod(CASTS.index(s), 4)
+                cast_w1(ca + 1, w1rest[ca + 1][:, :, piece * P:(piece + 1) * P], piece * 32, 32)
             if t == PACK - 1:
+                if u in (0, 2):
+                    quant_w1(u // 2 + 1)
                 if u == 1:
                     nc.vector.tensor_copy(v2s[:], tab2s[:].indirect(idx2[:]))
-                if u == 2:
-                    quant_w1(2)
                 if u == 3:
                     gather_v2(0, 0)
                     gather_v2(0, 1)

@@ -18,13 +18,19 @@ ACT = mybir.ActivationFunctionType
 
 P = 128
 PACK = 4
+QUADS = 4
 N = 512
 CHUNKS = H // N
 HALVES = S // N
 MT = S2 // P
-SC_COLS = [192, 192, 192, 192, 192, 176]
+PER_COLUMN = 16
+FAULT_HALF = S2 // 2
+CAST_PIECE = P
 LEAD = 3
-CASTS = [0, 1, 2, 3, 5, 6, 9, 10]
+
+WEAVE_BESIDE_CASTS = 192
+WEAVE_ALONE = 288
+WEAVE_LAST = 176
 
 
 def tile_list_bottle_fault_tracing_kernel(tc, tab_words, tab_scales, offs, tab2_words, tab2_scales, offs2,
@@ -34,235 +40,242 @@ def tile_list_bottle_fault_tracing_kernel(tc, tab_words, tab_scales, offs, tab2_
         lists = ctx.enter_context(tc.tile_pool(name="lists", bufs=1))
         keep = ctx.enter_context(tc.tile_pool(name="keep", bufs=1))
         ring = ctx.enter_context(tc.tile_pool(name="ring", bufs=2))
-        ring3 = ctx.enter_context(tc.tile_pool(name="ring3", bufs=5))
-        psab = ctx.enter_context(tc.psum_pool(name="psab", bufs=3))
-        pse = ctx.enter_context(tc.psum_pool(name="pse", bufs=1))
+        ahead = ctx.enter_context(tc.tile_pool(name="ahead", bufs=LEAD + 2))
+        stage1 = ctx.enter_context(tc.psum_pool(name="stage1", bufs=3))
+        stage2 = ctx.enter_context(tc.psum_pool(name="stage2", bufs=1))
+        tables = ctx.enter_context(tc.tile_pool(name="tables", bufs=1))
 
-        idx = lists.tile([P, S // 16], U16, name="idx")
-        idx2 = lists.tile([P, S2 // 16], U16, name="idx2")
-        p1 = lists.tile([P, NP // 16], U16, name="p1")
-        p2 = lists.tile([P, NP // 16], U16, name="p2")
+        idx = lists.tile([P, S // PER_COLUMN], U16, name="idx")
+        idx2 = lists.tile([P, S2 // PER_COLUMN], U16, name="idx2")
+        p1 = lists.tile([P, NP // PER_COLUMN], U16, name="p1")
+        p2 = lists.tile([P, NP // PER_COLUMN], U16, name="p2")
 
-        over = ctx.enter_context(tc.tile_pool(name="over", bufs=1))
-        tabs = keep.tile([P, T], U8, name="tabs", align_bytes=64)
-        w4raw = keep.tile([P, 2 * H], U8, name="w4raw", tag="w4raw", align_bytes=64)
-        warm = over.tile([P, 8], F32, name="warm", offset=0)
-        warm2 = keep.tile([P, 8], F32, name="warm2")
+        def entries(lst, first, count):
+            return lst[:, first // PER_COLUMN:(first + count) // PER_COLUMN]
 
-        nc.vector.memset(tabs[:].bitcast(I32), 0)
-        nc.gpsimd.memset(warm[:], 1.0)
-        nc.scalar.activation(warm2[:], warm[:], ACT.Abs_reciprocal_sqrt)
+        def load_scale_rows(dst, src, rows):
+            nc.vector.memset(dst[:].bitcast(I32), 0)
+            for q in range(QUADS):
+                nc.sync.dma_start(dst[32 * q:32 * q + rows, :].bitcast(I32), src(q).bitcast(I32))
 
-        w1v = w1.rearrange("(p j) c -> p j c", j=PACK)
-        w1first = [keep.tile([P, PACK, N // 2], F32, name=f"w1first{u}", tag=f"w1first{u}", align_bytes=64) for u in range(2)]
-        tabw = over.tile([P, T], I32, name="tabw", offset=0)
+        w1_rows = w1.rearrange("(p i) c -> p i c", i=PACK)
+        w4_raw = keep.tile([P, 2 * H], U8, name="w4_raw", tag="w4_raw", align_bytes=64)
+        w1_first = [keep.tile([P, PACK, N // 2], F32, name=f"w1_first{u}", tag=f"w1_first{u}", align_bytes=64)
+                    for u in range(2)]
+        base_raw = tables.tile([P, MT], F32, name="base_raw", offset=0)
+        v_scales_all = keep.tile([P, T], U8, name="v_scales_all", align_bytes=64)
 
-        nc.sync.dma_start(w4raw[:].bitcast(I32), w4_words[0].bitcast(I32))
+        nc.sync.dma_start(w4_raw[:].bitcast(I32), w4_words[0].bitcast(I32))
         nc.sync.dma_start(idx[:], offs)
         nc.sync.dma_start(idx2[:], offs2)
         nc.sync.dma_start(p1[:], pos1)
         nc.sync.dma_start(p2[:], pos2)
+        with nc.allow_non_contiguous_dma(reason="fault 128 m + p lies on partition p, column m"):
+            nc.sync.dma_start(base_raw[:], base.rearrange("(m p) -> p m", p=P))
         for u in range(2):
-            nc.sync.dma_start(w1first[u][:], w1v[:, :, u * (N // 2):(u + 1) * (N // 2)])
-        for q in range(4):
-            nc.sync.dma_start(tabs[32 * q:32 * q + 4, :].bitcast(I32), tab_scales[0, 4 * q:4 * q + 4, :].bitcast(I32))
-        nc.sync.dma_start(tabw[:], tab_words[0].rearrange("p n t -> p (n t)").bitcast(I32))
+            nc.sync.dma_start(w1_first[u][:], w1_rows[:, :, u * (N // 2):(u + 1) * (N // 2)])
+        load_scale_rows(v_scales_all, lambda q: tab_scales[0, PACK * q:PACK * (q + 1), :], PACK)
 
-        vs = [keep.tile([P, N], U8, name=f"vs{j}", align_bytes=64) for j in range(HALVES)]
-        vw = [keep.tile([P, N], U32, name=f"vw{j}", align_bytes=64) for j in range(HALVES)]
-        w4d = [keep.tile([P, 2 * N], U8, name=f"w4d{a}", align_bytes=64) for a in range(CHUNKS)]
-        w4sd = [keep.tile([P, N], U8, name=f"w4sd{a}", align_bytes=64) for a in range(CHUNKS)]
-        w1q = [keep.tile([P, N], U32, name=f"w1q{a}", align_bytes=64) for a in range(CHUNKS)]
-        w1s = [keep.tile([P, N], U8, name=f"w1s{a}", align_bytes=64) for a in range(CHUNKS)]
-        w1b = [keep.tile([P, PACK * N], BF16, name=f"w1b{a}", tag=f"w1b{a}", align_bytes=64) for a in range(CHUNKS)]
-        v2w = [[keep.tile([P, S2 // 2], U32, name=f"v2w{u}_{a}", align_bytes=64) for a in range(CHUNKS)]
-               for u in range(2)]
-        v2s = keep.tile([P, S2], U8, name="v2s", align_bytes=64)
-        hq = [[keep.tile([P, N], U32, name=f"hq{j}_{a}", align_bytes=64) for a in range(CHUNKS)] for j in range(HALVES)]
-        hs = [[keep.tile([P, N], U8, name=f"hs{j}_{a}", align_bytes=64) for a in range(CHUNKS)] for j in range(HALVES)]
-        scores = [keep.tile([P, S], F32, name=f"scores{m}", align_bytes=64) for m in range(MT)]
+        base_isqrt = keep.tile([P, MT], F32, name="base_isqrt")
+        base_inv = keep.tile([P, MT], F32, name="base_inv")
+        nc.scalar.activation(base_isqrt[:], base_raw[:], ACT.Abs_reciprocal_sqrt)
+        nc.scalar.activation(base_inv[:], base_isqrt[:], ACT.Square)
 
-        def deal_words(a):
-            nc.vector.tensor_copy(w4d[a][:].rearrange("p (t q b) -> p t q b", t=PACK, b=2),
-                                  w4raw[:, 2 * N * a:2 * N * (a + 1)].rearrange("p (q t b) -> p t q b", t=PACK, b=2))
+        v_words_all = tables.tile([P, T], I32, name="v_words_all", offset=0)
+        nc.sync.dma_start(v_words_all[:], tab_words[0].rearrange("p n i -> p (n i)").bitcast(I32))
 
-        def deal_scales(a):
-            nc.vector.tensor_copy(w4sd[a][:].rearrange("p (t q) -> p t q", t=PACK),
-                                  w4sraw[:, N * a:N * (a + 1)].rearrange("p (q t) -> p t q", t=PACK))
+        def operand(name, count, width, dtype):
+            return [keep.tile([P, width], dtype, name=f"{name}{c}", tag=f"{name}{c}", align_bytes=64)
+                    for c in range(count)]
 
-        def cast_w1(a, raw, m0, mn):
-            dst = w1b[a][:].rearrange("p (t m j) -> p m j t", t=PACK, j=PACK)[:, m0:m0 + mn]
-            nc.scalar.copy(dst, raw.rearrange("p j (m t) -> p m j t", t=PACK))
+        v_scales = operand("v_scales", HALVES, N, U8)
+        v_words = operand("v_words", HALVES, N, U32)
+        w4_codes = operand("w4_codes", CHUNKS, 2 * N, U8)
+        w4_scale = operand("w4_scale", CHUNKS, N, U8)
+        w1_codes = operand("w1_codes", CHUNKS, N, U32)
+        w1_scale = operand("w1_scale", CHUNKS, N, U8)
+        w1_bf16 = operand("w1_bf16", CHUNKS, PACK * N, BF16)
+        v2_words = [[tile[:] for tile in operand("v2_words", CHUNKS, FAULT_HALF, U32)]]
+        v2_scales = keep.tile([P, S2], U8, name="v2_scales", align_bytes=64)
+        h_codes = [operand(f"h_codes{j}_", CHUNKS, N, U32) for j in range(HALVES)]
+        h_scale = [operand(f"h_scale{j}_", CHUNKS, N, U8) for j in range(HALVES)]
+        scores = operand("scores", MT, S, F32)
 
-        def quant_w1(a):
-            nc.vector.quantize_mx(out=w1q[a][:].bitcast(FP8X4), scales=w1s[a][:], in_=w1b[a][:])
+        def deal_w4_codes(a):
+            nc.vector.tensor_copy(w4_codes[a][:].rearrange("p (t q b) -> p t q b", t=PACK, b=2),
+                                  w4_raw[:, 2 * N * a:2 * N * (a + 1)].rearrange("p (q t b) -> p t q b", t=PACK, b=2))
 
-        def gather_v2(u, a):
-            nc.vector.tensor_copy(v2w[u][a][:], tab2w[:, a * T3:(a + 1) * T3].bitcast(U32).indirect(idx2[:, 16 * u:16 * (u + 1)]))
+        def deal_w4_scale(a):
+            nc.vector.tensor_copy(w4_scale[a][:].rearrange("p (t q) -> p t q", t=PACK),
+                                  w4_scale_raw[:, N * a:N * (a + 1)].rearrange("p (q t) -> p t q", t=PACK))
+
+        def cast_w1(a, raw, first):
+            q0, count = first // PACK, raw.shape[2] // PACK
+            dst = w1_bf16[a][:].rearrange("p (t q i) -> p q i t", t=PACK, i=PACK)[:, q0:q0 + count]
+            nc.scalar.copy(dst, raw.rearrange("p i (q t) -> p q i t", t=PACK))
+
+        def quantise_w1(a):
+            nc.vector.quantize_mx(out=w1_codes[a][:].bitcast(FP8X4), scales=w1_scale[a][:], in_=w1_bf16[a][:])
+
+        def gather_v2_words(half, a):
+            window = v2_words_all[:, a * T3:(a + 1) * T3].bitcast(U32)
+            nc.vector.tensor_copy(v2_words[half][a], window.indirect(entries(idx2, half * FAULT_HALF, FAULT_HALF)))
 
         for a in range(CHUNKS):
-            deal_words(a)
-        w4sraw = keep.tile([P, H], U8, name="w4sraw", tag="w4raw", align_bytes=64)
-        nc.vector.memset(w4sraw[:].bitcast(I32), 0)
-        for q in range(4):
-            nc.sync.dma_start(w4sraw[32 * q:32 * q + 4, :].bitcast(I32), w4_scales[0, 4 * q:4 * q + 4, :].bitcast(I32))
+            deal_w4_codes(a)
+        w4_scale_raw = keep.tile([P, H], U8, name="w4_scale_raw", tag="w4_raw", align_bytes=64)
+        load_scale_rows(w4_scale_raw, lambda q: w4_scales[0, PACK * q:PACK * (q + 1), :], PACK)
         for u in range(2):
-            cast_w1(0, w1first[u][:], u * 64, 64)
-        capt = keep.tile([P, CHUNKS, PACK], F32, name="capt", tag="w1first0", align_bytes=64)
-        nc.sync.dma_start(capt[:], cap.rearrange("(a p t) -> p a t", p=P, t=PACK))
-        quant_w1(0)
-        w1rest = {a: keep.tile([P, PACK, N], F32, name=f"w1rest{a}", tag=tag, align_bytes=64)
-                  for a, tag in ((1, "w1first1"), (2, "w1b0"))}
-        for a in w1rest:
-            nc.sync.dma_start(w1rest[a][:], w1v[:, :, a * N:(a + 1) * N])
+            cast_w1(0, w1_first[u][:], u * (N // 2))
+        caps = keep.tile([P, CHUNKS, PACK], F32, name="caps", tag="w1_first0", align_bytes=64)
+        nc.sync.dma_start(caps[:], cap.rearrange("(a p t) -> p a t", p=P, t=PACK))
+        quantise_w1(0)
+        w1_later = {a: keep.tile([P, PACK, N], F32, name=f"w1_later{a}", tag=tag, align_bytes=64)
+                    for a, tag in ((1, "w1_first1"), (2, "w1_bf160"))}
+        for a in w1_later:
+            nc.sync.dma_start(w1_later[a][:], w1_rows[:, :, a * N:(a + 1) * N])
         for j in range(HALVES):
-            nc.vector.tensor_copy(vs[j][:], tabs[:].indirect(idx[:, 32 * j:32 * (j + 1)]))
+            nc.vector.tensor_copy(v_scales[j][:], v_scales_all[:].indirect(entries(idx, j * N, N)))
         for j in range(HALVES):
-            nc.vector.tensor_copy(vw[j][:], tabw[:].bitcast(U32).indirect(idx[:, 32 * j:32 * (j + 1)]))
+            nc.vector.tensor_copy(v_words[j][:], v_words_all[:].bitcast(U32).indirect(entries(idx, j * N, N)))
             if j == 0:
-                deal_scales(0)
+                deal_w4_scale(0)
         for a in range(1, CHUNKS):
-            deal_scales(a)
+            deal_w4_scale(a)
 
-        tab2s = over.tile([P, T3], U8, name="tab2s", offset=0)
-        tab2w = over.tile([P, CHUNKS * T3], I32, name="tab2w", offset=T3 + 64)
-        nc.vector.memset(tab2s[:].bitcast(I32), 0)
-        for q in range(4):
-            nc.sync.dma_start(tab2s[32 * q:32 * q + 4 * CHUNKS, :].bitcast(I32),
-                              tab2_scales[:, 4 * q:4 * q + 4, :].bitcast(I32))
-        nc.sync.dma_start(tab2w[:].rearrange("p (a n) -> p a n", a=CHUNKS),
-                          tab2_words.rearrange("a p n t -> p a (n t)").bitcast(I32))
-        baset = over.tile([P, MT], F32, name="baset", offset=T3)
-        with nc.allow_non_contiguous_dma(reason="one value a partition"):
-            nc.sync.dma_start(baset[:], base.rearrange("(m p) -> p m", p=P))
+        v2_scales_all = tables.tile([P, T3], U8, name="v2_scales_all", offset=0)
+        v2_words_all = tables.tile([P, CHUNKS * T3], I32, name="v2_words_all", offset=T3)
+        load_scale_rows(v2_scales_all, lambda q: tab2_scales[:, PACK * q:PACK * (q + 1), :], PACK * CHUNKS)
+        nc.sync.dma_start(v2_words_all[:].rearrange("p (a n) -> p a n", a=CHUNKS),
+                          tab2_words.rearrange("a p n i -> p a (n i)").bitcast(I32))
 
         units = [(j, a) for a in range(CHUNKS) for j in range(HALVES)]
         steps = [(j, a, t) for j, a in units for t in range(PACK)]
-        mags, hbs, his, banks = {}, {}, {}, {}
+        last = len(units) - 1
+        magnitudes, h_rows, h_woven, banks = {}, {}, {}, {}
 
         def contrast(s):
             j, a, t = steps[s]
-            pa = psab.tile([P, N], F32, name="pa")
-            nc.tensor.matmul_mx(out=pa[:], lhsT=w1q[a][:, t * P:(t + 1) * P].bitcast(FP8X4),
-                                lhsT_scale=w1s[a][:, t * P:(t + 1) * P],
-                                rhs=vw[j][:].bitcast(FP8X4), rhs_scale=vs[j][:],
-                                start=True, stop=True)
-            mags[s] = ring3.tile([P, N], F32, name="mag")
-            nc.scalar.activation(mags[s][:], pa[:], ACT.Abs)
+            bank = stage1.tile([P, N], F32, name="w1_product")
+            nc.tensor.matmul_mx(out=bank[:], lhsT=w1_codes[a][:, t * P:(t + 1) * P].bitcast(FP8X4),
+                                lhsT_scale=w1_scale[a][:, t * P:(t + 1) * P],
+                                rhs=v_words[j][:].bitcast(FP8X4), rhs_scale=v_scales[j][:], start=True, stop=True)
+            magnitudes[s] = ahead.tile([P, N], F32, name="magnitude")
+            nc.scalar.activation(magnitudes[s][:], bank[:], ACT.Abs)
 
         def residual(s):
             j, a, t = steps[s]
             if t == 0:
-                hbs[j, a] = ring.tile([P, PACK, N], BF16, name="hb", align_bytes=64)
-            pb = psab.tile([P, N], F32, name="pb")
-            nc.tensor.matmul_mx(out=pb[:], lhsT=w4d[a][:, 2 * t * P:2 * (t + 1) * P].bitcast(FP4X4),
-                                lhsT_scale=w4sd[a][:, t * P:(t + 1) * P],
-                                rhs=vw[j][:].bitcast(FP8X4), rhs_scale=vs[j][:],
-                                start=True, stop=True)
-            nc.vector.scalar_tensor_tensor(hbs[j, a][:, t, :], mags[s][:], capt[:, a, t:t + 1], pb[:],
+                h_rows[j, a] = ring.tile([P, PACK, N], BF16, name="h_rows", tag="h_rows", align_bytes=64)
+            bank = stage1.tile([P, N], F32, name="w4_product")
+            nc.tensor.matmul_mx(out=bank[:], lhsT=w4_codes[a][:, 2 * t * P:2 * (t + 1) * P].bitcast(FP4X4),
+                                lhsT_scale=w4_scale[a][:, t * P:(t + 1) * P],
+                                rhs=v_words[j][:].bitcast(FP8X4), rhs_scale=v_scales[j][:], start=True, stop=True)
+            nc.vector.scalar_tensor_tensor(h_rows[j, a][:, t, :], magnitudes[s][:], caps[:, a, t:t + 1], bank[:],
                                            ALU.min, ALU.add)
 
-        def weave(eng, u):
-            j, a = units[u]
-            if (j, a) not in his:
-                his[j, a] = keep.tile([P, N, PACK], BF16, name="hi" if u + 1 < len(units) else "hi_last",
-                                      align_bytes=64)
-            src = hbs[j, a][:].rearrange("p t (c i) -> p c t i", i=4)
-            dst = his[j, a][:].rearrange("p (c i) t -> p c t i", i=4)
-            cut = SC_COLS[u] // 4
-            if eng == "s":
-                if cut > 0:
-                    nc.scalar.copy(dst[:, 0:cut], src[:, 0:cut])
-            elif eng == "v":
-                nc.vector.tensor_copy(dst[:, cut:N // 4], src[:, cut:N // 4])
-            else:
-                nc.gpsimd.tensor_scalar(his[j, a][:, 4 * cut:N, :],
-                                        hbs[j, a][:].rearrange("p t n -> p n t")[:, 4 * cut:N, :],
-                                        1.0, 0.0, ALU.mult, ALU.add)
+        def by_fours(u, first, end):
+            src = h_rows[units[u]][:].rearrange("p t (c i) -> p c t i", i=4)
+            dst = h_woven[u][:].rearrange("p (c i) t -> p c t i", i=4)
+            return dst[:, first // 4:end // 4], src[:, first // 4:end // 4]
 
-        def quant_h(u):
+        def weave(u):
+            cut = WEAVE_BESIDE_CASTS if u < 2 else WEAVE_ALONE
+            h_woven[u] = keep.tile([P, N, PACK], BF16, name="h_woven", align_bytes=64)
+            nc.gpsimd.tensor_scalar(h_woven[u][:, cut:N, :],
+                                    h_rows[units[u]][:].rearrange("p t n -> p n t")[:, cut:N, :],
+                                    1.0, 0.0, ALU.mult, ALU.add)
+            nc.scalar.copy(*by_fours(u, 0, cut))
+
+        def weave_last():
+            h_woven[last] = keep.tile([P, N, PACK], BF16, name="h_woven_last", align_bytes=64)
+            nc.scalar.copy(*by_fours(last, 0, WEAVE_LAST))
+            nc.vector.tensor_copy(*by_fours(last, WEAVE_LAST, N))
+
+        def quantise_h(u):
             j, a = units[u]
-            nc.vector.quantize_mx(out=hq[j][a][:].bitcast(FP8X4), scales=hs[j][a][:],
-                                  in_=his[j, a][:].rearrange("p n t -> p (n t)"))
+            nc.vector.quantize_mx(out=h_codes[j][a][:].bitcast(FP8X4), scales=h_scale[j][a][:],
+                                  in_=h_woven[u][:].rearrange("p n t -> p (n t)"))
 
         def score_pass(j, a, m):
             if a == 0:
-                banks[j, m] = pse.tile([P, N], F32, name=f"e{j}")
-            u, c = divmod(m * P, S2 // 2)
-            nc.tensor.matmul_mx(out=banks[j, m][:], lhsT=v2w[u][a][:, c:c + P].bitcast(FP8X4),
-                                lhsT_scale=v2s[4 * a:P, m * P:(m + 1) * P],
-                                rhs=hq[j][a][:].bitcast(FP8X4), rhs_scale=hs[j][a][:],
+                banks[j, m] = stage2.tile([P, N], F32, name=f"score_bank{j}")
+            half, first = divmod(m * P, FAULT_HALF)
+            nc.tensor.matmul_mx(out=banks[j, m][:], lhsT=v2_words[half][a][:, first:first + P].bitcast(FP8X4),
+                                lhsT_scale=v2_scales[PACK * a:P, m * P:(m + 1) * P],
+                                rhs=h_codes[j][a][:].bitcast(FP8X4), rhs_scale=h_scale[j][a][:],
                                 start=(a == 0), stop=(a == CHUNKS - 1))
             if a == CHUNKS - 1:
                 nc.scalar.copy(scores[m][:, j * N:(j + 1) * N], banks[j, m][:])
+
+        def cast_piece(a, piece):
+            first = piece * CAST_PIECE
+            cast_w1(a, w1_later[a][:, :, first:first + CAST_PIECE], first)
 
         for s in range(LEAD):
             contrast(s)
         for s in range(len(steps)):
             u, t = divmod(s, PACK)
-            j, a = units[u]
             if s + LEAD < len(steps):
                 contrast(s + LEAD)
             if u > 0 and t == 0:
-                weave("g", u - 1)
-                weave("s", u - 1)
+                weave(u - 1)
             residual(s)
-            if s in CASTS:
-                ca, piece = divmod(CASTS.index(s), 4)
-                cast_w1(ca + 1, w1rest[ca + 1][:, :, piece * P:(piece + 1) * P], piece * 32, 32)
+            if u == 0:
+                cast_piece(1, t)
+            elif u <= 2 and t in (1, 2):
+                cast_piece(2, 2 * (u - 1) + t - 1)
             if t == PACK - 1:
                 if u in (0, 2):
-                    quant_w1(u // 2 + 1)
+                    quantise_w1(u // 2 + 1)
                 if u == 1:
-                    nc.vector.tensor_copy(v2s[:], tab2s[:].indirect(idx2[:]))
-                if u == 3:
-                    gather_v2(0, 0)
-                    gather_v2(0, 1)
-                if u == 4:
-                    gather_v2(0, 2)
+                    nc.vector.tensor_copy(v2_scales[:], v2_scales_all[:].indirect(idx2[:]))
+                a2 = u - (last + 1 - CHUNKS)
+                if a2 >= 0:
+                    gather_v2_words(0, a2)
                 if u > 0:
-                    quant_h(u - 1)
-                if u == 3:
-                    score_pass(0, 0, 0)
-                    score_pass(1, 0, 0)
-                    score_pass(0, 1, 0)
-                if u == 4:
-                    score_pass(1, 1, 0)
-                if u == 5:
-                    score_pass(0, 2, 0)
-        last = len(units) - 1
-        weave("s", last)
-        weave("v", last)
-        gather_v2(1, 0)
-        quant_h(last)
+                    quantise_h(u - 1)
+                if a2 >= 0:
+                    score_pass(0, a2, 0)
+                    if u < last:
+                        score_pass(1, a2, 0)
+
+        weave_last()
+        late = ring.tile([P, CHUNKS * FAULT_HALF], U32, name="v2_words_late", tag="h_rows", align_bytes=64)
+        v2_words.append([late[:, a * FAULT_HALF:(a + 1) * FAULT_HALF] for a in range(CHUNKS)])
+        gather_v2_words(1, 0)
+        quantise_h(last)
         score_pass(1, CHUNKS - 1, 0)
         for a in range(1, CHUNKS):
-            gather_v2(1, a)
+            gather_v2_words(1, a)
 
-        tiles = {}
+        shoulders = {}
 
         def shoulder(m):
             e1 = ring.tile([P, NP], F32, name="e1")
-            mag1 = ring.tile([P, NP], F32, name="mag1")
+            ratio = ring.tile([P, NP], F32, name="ratio")
             root = ring.tile([P, NP], F32, name="root")
-            inv = ring.tile([P, NP], F32, name="inv")
+            inverse = ring.tile([P, NP], F32, name="inverse")
             nc.vector.tensor_copy(e1[:], scores[m][:].indirect(p1[:]))
-            nc.scalar.activation(mag1[:], e1[:], ACT.Abs)
-            nc.scalar.activation(root[:], mag1[:], ACT.Abs_reciprocal_sqrt, bias=baset[:, m:m + 1])
-            nc.scalar.activation(inv[:], root[:], ACT.Square)
-            tiles[m] = (e1, inv)
+            nc.scalar.activation(ratio[:], e1[:], ACT.Abs, scale=base_inv[:, m:m + 1])
+            nc.scalar.activation(root[:], ratio[:], ACT.Abs_reciprocal_sqrt, bias=1.0)
+            nc.scalar.activation(inverse[:], root[:], ACT.Square, scale=base_isqrt[:, m:m + 1])
+            shoulders[m] = (e1, inverse)
 
         shoulder(0)
         for m in range(MT):
-            e1, inv = tiles[m]
-            tot = ring.tile([P, NP], F32, name="tot")
-            res = ring.tile([P, NP], F32, name="res")
+            e1, inverse = shoulders[m]
+            total = ring.tile([P, NP], F32, name="total")
+            result = ring.tile([P, NP], F32, name="result")
             if m + 1 < MT:
                 for j in range(HALVES):
                     for a in range(CHUNKS):
                         score_pass(j, a, m + 1)
-            nc.vector.tensor_tensor(tot[:], scores[m][:].indirect(p2[:]), e1[:], ALU.add)
+            nc.vector.tensor_tensor(total[:], scores[m][:].indirect(p2[:]), e1[:], ALU.add)
             if m + 1 < MT:
                 shoulder(m + 1)
-            nc.vector.tensor_tensor(res[:], tot[:], inv[:], ALU.mult)
-            nc.sync.dma_start(out[m * P:(m + 1) * P, :], res[:])
+            parts = 2 if m + 1 == MT else 1
+            for k in range(parts):
+                cols = slice(k * NP // parts, (k + 1) * NP // parts)
+                nc.vector.tensor_tensor(result[:, cols], total[:, cols], inverse[:, cols], ALU.mult)
+                nc.sync.dma_start(out[m * P:(m + 1) * P, cols], result[:, cols])

from contextlib import ExitStack

import concourse.mybir as mybir

K, H, T, S, S2, T3, NP = 512, 1536, 4096, 1024, 512, 2048, 512
FLOPS = 2 * (2 * K * H * S + H * S2 * S)

F32 = mybir.dt.float32
BF16 = mybir.dt.bfloat16
I32 = mybir.dt.int32
U32 = mybir.dt.uint32
U16 = mybir.dt.uint16
U8 = mybir.dt.uint8
FP8X4 = mybir.dt.float8_e4m3fn_x4
FP4X4 = mybir.dt.float4_e2m1fn_x4
ALU = mybir.AluOpType
ACT = mybir.ActivationFunctionType

P = 128
PACK = 4
QUADS = 4
N = 512
CHUNKS = H // N
HALVES = S // N
MT = S2 // P
PER_COLUMN = 16
FAULT_HALF = S2 // 2
CAST_PIECE = P
LEAD = 3

WEAVE_BESIDE_CASTS = 192
WEAVE_ALONE = 288
WEAVE_LAST = 176


def tile_list_bottle_fault_tracing_kernel(tc, tab_words, tab_scales, offs, tab2_words, tab2_scales, offs2,
                                                   pos1, pos2, w1, w4_words, w4_scales, cap, base, out):
    nc = tc.nc
    with ExitStack() as ctx:
        lists = ctx.enter_context(tc.tile_pool(name="lists", bufs=1))
        keep = ctx.enter_context(tc.tile_pool(name="keep", bufs=1))
        ring = ctx.enter_context(tc.tile_pool(name="ring", bufs=2))
        ahead = ctx.enter_context(tc.tile_pool(name="ahead", bufs=LEAD + 2))
        stage1 = ctx.enter_context(tc.psum_pool(name="stage1", bufs=3))
        stage2 = ctx.enter_context(tc.psum_pool(name="stage2", bufs=1))
        tables = ctx.enter_context(tc.tile_pool(name="tables", bufs=1))

        idx = lists.tile([P, S // PER_COLUMN], U16, name="idx")
        idx2 = lists.tile([P, S2 // PER_COLUMN], U16, name="idx2")
        p1 = lists.tile([P, NP // PER_COLUMN], U16, name="p1")
        p2 = lists.tile([P, NP // PER_COLUMN], U16, name="p2")

        def entries(lst, first, count):
            return lst[:, first // PER_COLUMN:(first + count) // PER_COLUMN]

        def load_scale_rows(dst, src, rows):
            nc.vector.memset(dst[:].bitcast(I32), 0)
            for q in range(QUADS):
                nc.sync.dma_start(dst[32 * q:32 * q + rows, :].bitcast(I32), src(q).bitcast(I32))

        w1_rows = w1.rearrange("(p i) c -> p i c", i=PACK)
        w4_raw = keep.tile([P, 2 * H], U8, name="w4_raw", tag="w4_raw", align_bytes=64)
        w1_first = [keep.tile([P, PACK, N // 2], F32, name=f"w1_first{u}", tag=f"w1_first{u}", align_bytes=64)
                    for u in range(2)]
        base_raw = tables.tile([P, MT], F32, name="base_raw", offset=0)
        v_scales_all = keep.tile([P, T], U8, name="v_scales_all", align_bytes=64)

        nc.sync.dma_start(w4_raw[:].bitcast(I32), w4_words[0].bitcast(I32))
        nc.sync.dma_start(idx[:], offs)
        nc.sync.dma_start(idx2[:], offs2)
        nc.sync.dma_start(p1[:], pos1)
        nc.sync.dma_start(p2[:], pos2)
        with nc.allow_non_contiguous_dma(reason="fault 128 m + p lies on partition p, column m"):
            nc.sync.dma_start(base_raw[:], base.rearrange("(m p) -> p m", p=P))
        for u in range(2):
            nc.sync.dma_start(w1_first[u][:], w1_rows[:, :, u * (N // 2):(u + 1) * (N // 2)])
        load_scale_rows(v_scales_all, lambda q: tab_scales[0, PACK * q:PACK * (q + 1), :], PACK)

        base_isqrt = keep.tile([P, MT], F32, name="base_isqrt")
        base_inv = keep.tile([P, MT], F32, name="base_inv")
        nc.scalar.activation(base_isqrt[:], base_raw[:], ACT.Abs_reciprocal_sqrt)
        nc.scalar.activation(base_inv[:], base_isqrt[:], ACT.Square)

        v_words_all = tables.tile([P, T], I32, name="v_words_all", offset=0)
        nc.sync.dma_start(v_words_all[:], tab_words[0].rearrange("p n i -> p (n i)").bitcast(I32))

        def operand(name, count, width, dtype):
            return [keep.tile([P, width], dtype, name=f"{name}{c}", tag=f"{name}{c}", align_bytes=64)
                    for c in range(count)]

        v_scales = operand("v_scales", HALVES, N, U8)
        v_words = operand("v_words", HALVES, N, U32)
        w4_codes = operand("w4_codes", CHUNKS, 2 * N, U8)
        w4_scale = operand("w4_scale", CHUNKS, N, U8)
        w1_codes = operand("w1_codes", CHUNKS, N, U32)
        w1_scale = operand("w1_scale", CHUNKS, N, U8)
        w1_bf16 = operand("w1_bf16", CHUNKS, PACK * N, BF16)
        v2_words = [[tile[:] for tile in operand("v2_words", CHUNKS, FAULT_HALF, U32)]]
        v2_scales = keep.tile([P, S2], U8, name="v2_scales", align_bytes=64)
        h_codes = [operand(f"h_codes{j}_", CHUNKS, N, U32) for j in range(HALVES)]
        h_scale = [operand(f"h_scale{j}_", CHUNKS, N, U8) for j in range(HALVES)]
        scores = operand("scores", MT, S, F32)

        def deal_w4_codes(a):
            nc.vector.tensor_copy(w4_codes[a][:].rearrange("p (t q b) -> p t q b", t=PACK, b=2),
                                  w4_raw[:, 2 * N * a:2 * N * (a + 1)].rearrange("p (q t b) -> p t q b", t=PACK, b=2))

        def deal_w4_scale(a):
            nc.vector.tensor_copy(w4_scale[a][:].rearrange("p (t q) -> p t q", t=PACK),
                                  w4_scale_raw[:, N * a:N * (a + 1)].rearrange("p (q t) -> p t q", t=PACK))

        def cast_w1(a, raw, first):
            q0, count = first // PACK, raw.shape[2] // PACK
            dst = w1_bf16[a][:].rearrange("p (t q i) -> p q i t", t=PACK, i=PACK)[:, q0:q0 + count]
            nc.scalar.copy(dst, raw.rearrange("p i (q t) -> p q i t", t=PACK))

        def quantise_w1(a):
            nc.vector.quantize_mx(out=w1_codes[a][:].bitcast(FP8X4), scales=w1_scale[a][:], in_=w1_bf16[a][:])

        def gather_v2_words(half, a):
            window = v2_words_all[:, a * T3:(a + 1) * T3].bitcast(U32)
            nc.vector.tensor_copy(v2_words[half][a], window.indirect(entries(idx2, half * FAULT_HALF, FAULT_HALF)))

        for a in range(CHUNKS):
            deal_w4_codes(a)
        w4_scale_raw = keep.tile([P, H], U8, name="w4_scale_raw", tag="w4_raw", align_bytes=64)
        load_scale_rows(w4_scale_raw, lambda q: w4_scales[0, PACK * q:PACK * (q + 1), :], PACK)
        for u in range(2):
            cast_w1(0, w1_first[u][:], u * (N // 2))
        caps = keep.tile([P, CHUNKS, PACK], F32, name="caps", tag="w1_first0", align_bytes=64)
        nc.sync.dma_start(caps[:], cap.rearrange("(a p t) -> p a t", p=P, t=PACK))
        quantise_w1(0)
        w1_later = {a: keep.tile([P, PACK, N], F32, name=f"w1_later{a}", tag=tag, align_bytes=64)
                    for a, tag in ((1, "w1_first1"), (2, "w1_bf160"))}
        for a in w1_later:
            nc.sync.dma_start(w1_later[a][:], w1_rows[:, :, a * N:(a + 1) * N])
        for j in range(HALVES):
            nc.vector.tensor_copy(v_scales[j][:], v_scales_all[:].indirect(entries(idx, j * N, N)))
        for j in range(HALVES):
            nc.vector.tensor_copy(v_words[j][:], v_words_all[:].bitcast(U32).indirect(entries(idx, j * N, N)))
            if j == 0:
                deal_w4_scale(0)
        for a in range(1, CHUNKS):
            deal_w4_scale(a)

        v2_scales_all = tables.tile([P, T3], U8, name="v2_scales_all", offset=0)
        v2_words_all = tables.tile([P, CHUNKS * T3], I32, name="v2_words_all", offset=T3)
        load_scale_rows(v2_scales_all, lambda q: tab2_scales[:, PACK * q:PACK * (q + 1), :], PACK * CHUNKS)
        nc.sync.dma_start(v2_words_all[:].rearrange("p (a n) -> p a n", a=CHUNKS),
                          tab2_words.rearrange("a p n i -> p a (n i)").bitcast(I32))

        units = [(j, a) for a in range(CHUNKS) for j in range(HALVES)]
        steps = [(j, a, t) for j, a in units for t in range(PACK)]
        last = len(units) - 1
        magnitudes, h_rows, h_woven, banks = {}, {}, {}, {}

        def contrast(s):
            j, a, t = steps[s]
            bank = stage1.tile([P, N], F32, name="w1_product")
            nc.tensor.matmul_mx(out=bank[:], lhsT=w1_codes[a][:, t * P:(t + 1) * P].bitcast(FP8X4),
                                lhsT_scale=w1_scale[a][:, t * P:(t + 1) * P],
                                rhs=v_words[j][:].bitcast(FP8X4), rhs_scale=v_scales[j][:], start=True, stop=True)
            magnitudes[s] = ahead.tile([P, N], F32, name="magnitude")
            nc.scalar.activation(magnitudes[s][:], bank[:], ACT.Abs)

        def residual(s):
            j, a, t = steps[s]
            if t == 0:
                h_rows[j, a] = ring.tile([P, PACK, N], BF16, name="h_rows", tag="h_rows", align_bytes=64)
            bank = stage1.tile([P, N], F32, name="w4_product")
            nc.tensor.matmul_mx(out=bank[:], lhsT=w4_codes[a][:, 2 * t * P:2 * (t + 1) * P].bitcast(FP4X4),
                                lhsT_scale=w4_scale[a][:, t * P:(t + 1) * P],
                                rhs=v_words[j][:].bitcast(FP8X4), rhs_scale=v_scales[j][:], start=True, stop=True)
            nc.vector.scalar_tensor_tensor(h_rows[j, a][:, t, :], magnitudes[s][:], caps[:, a, t:t + 1], bank[:],
                                           ALU.min, ALU.add)

        def by_fours(u, first, end):
            src = h_rows[units[u]][:].rearrange("p t (c i) -> p c t i", i=4)
            dst = h_woven[u][:].rearrange("p (c i) t -> p c t i", i=4)
            return dst[:, first // 4:end // 4], src[:, first // 4:end // 4]

        def weave(u):
            cut = WEAVE_BESIDE_CASTS if u < 2 else WEAVE_ALONE
            h_woven[u] = keep.tile([P, N, PACK], BF16, name="h_woven", align_bytes=64)
            nc.gpsimd.tensor_scalar(h_woven[u][:, cut:N, :],
                                    h_rows[units[u]][:].rearrange("p t n -> p n t")[:, cut:N, :],
                                    1.0, 0.0, ALU.mult, ALU.add)
            nc.scalar.copy(*by_fours(u, 0, cut))

        def weave_last():
            h_woven[last] = keep.tile([P, N, PACK], BF16, name="h_woven_last", align_bytes=64)
            nc.scalar.copy(*by_fours(last, 0, WEAVE_LAST))
            nc.vector.tensor_copy(*by_fours(last, WEAVE_LAST, N))

        def quantise_h(u):
            j, a = units[u]
            nc.vector.quantize_mx(out=h_codes[j][a][:].bitcast(FP8X4), scales=h_scale[j][a][:],
                                  in_=h_woven[u][:].rearrange("p n t -> p (n t)"))

        def score_pass(j, a, m):
            if a == 0:
                banks[j, m] = stage2.tile([P, N], F32, name=f"score_bank{j}")
            half, first = divmod(m * P, FAULT_HALF)
            nc.tensor.matmul_mx(out=banks[j, m][:], lhsT=v2_words[half][a][:, first:first + P].bitcast(FP8X4),
                                lhsT_scale=v2_scales[PACK * a:P, m * P:(m + 1) * P],
                                rhs=h_codes[j][a][:].bitcast(FP8X4), rhs_scale=h_scale[j][a][:],
                                start=(a == 0), stop=(a == CHUNKS - 1))
            if a == CHUNKS - 1:
                nc.scalar.copy(scores[m][:, j * N:(j + 1) * N], banks[j, m][:])

        def cast_piece(a, piece):
            first = piece * CAST_PIECE
            cast_w1(a, w1_later[a][:, :, first:first + CAST_PIECE], first)

        for s in range(LEAD):
            contrast(s)
        for s in range(len(steps)):
            u, t = divmod(s, PACK)
            if s + LEAD < len(steps):
                contrast(s + LEAD)
            if u > 0 and t == 0:
                weave(u - 1)
            residual(s)
            if u == 0:
                cast_piece(1, t)
            elif u <= 2 and t in (1, 2):
                cast_piece(2, 2 * (u - 1) + t - 1)
            if t == PACK - 1:
                if u in (0, 2):
                    quantise_w1(u // 2 + 1)
                if u == 1:
                    nc.vector.tensor_copy(v2_scales[:], v2_scales_all[:].indirect(idx2[:]))
                a2 = u - (last + 1 - CHUNKS)
                if a2 >= 0:
                    gather_v2_words(0, a2)
                if u > 0:
                    quantise_h(u - 1)
                if a2 >= 0:
                    score_pass(0, a2, 0)
                    if u < last:
                        score_pass(1, a2, 0)

        weave_last()
        late = ring.tile([P, CHUNKS * FAULT_HALF], U32, name="v2_words_late", tag="h_rows", align_bytes=64)
        v2_words.append([late[:, a * FAULT_HALF:(a + 1) * FAULT_HALF] for a in range(CHUNKS)])
        gather_v2_words(1, 0)
        quantise_h(last)
        score_pass(1, CHUNKS - 1, 0)
        for a in range(1, CHUNKS):
            gather_v2_words(1, a)

        shoulders = {}

        def shoulder(m):
            e1 = ring.tile([P, NP], F32, name="e1")
            ratio = ring.tile([P, NP], F32, name="ratio")
            root = ring.tile([P, NP], F32, name="root")
            inverse = ring.tile([P, NP], F32, name="inverse")
            nc.vector.tensor_copy(e1[:], scores[m][:].indirect(p1[:]))
            nc.scalar.activation(ratio[:], e1[:], ACT.Abs, scale=base_inv[:, m:m + 1])
            nc.scalar.activation(root[:], ratio[:], ACT.Abs_reciprocal_sqrt, bias=1.0)
            nc.scalar.activation(inverse[:], root[:], ACT.Square, scale=base_isqrt[:, m:m + 1])
            shoulders[m] = (e1, inverse)

        shoulder(0)
        for m in range(MT):
            e1, inverse = shoulders[m]
            total = ring.tile([P, NP], F32, name="total")
            result = ring.tile([P, NP], F32, name="result")
            if m + 1 < MT:
                for j in range(HALVES):
                    for a in range(CHUNKS):
                        score_pass(j, a, m + 1)
            nc.vector.tensor_tensor(total[:], scores[m][:].indirect(p2[:]), e1[:], ALU.add)
            if m + 1 < MT:
                shoulder(m + 1)
            parts = 2 if m + 1 == MT else 1
            for k in range(parts):
                cols = slice(k * NP // parts, (k + 1) * NP // parts)
                nc.vector.tensor_tensor(result[:, cols], total[:, cols], inverse[:, cols], ALU.mult)
                nc.sync.dma_start(out[m * P:(m + 1) * P, cols], result[:, cols])
